import numpy as np, ml_dtypes
CORES = [16,17,18,19,150,151]
N = 6
import mx_ref
NC, G = 256, 4
C = np.float32(0.043)
CNT = [[0,72,104,0,80,0],[0,8,120,56,72,0],[0,0,32,56,0,168],[144,0,0,104,8,0],[104,40,0,40,56,16],[8,136,0,0,40,72]]
OFF = [[sum(c[:e]) for e in range(N + 1)] for c in CNT]
BF = ml_dtypes.bfloat16
def cut(t, i, w=512):
    return t[:, w * i:w * i + w]
def tile(rs):
    return np.stack(rs, axis=2).reshape(128, -1).astype(BF)
def layer(w, X):
    out = []
    for i in range(G):
        for t in range(len(X)):
            p = mx_ref.matmul(mx_ref.quantize(cut(w, len(X) * i + t)), X[t])
            z = p if t == 0 else z + p
        out.append(z)
    return out
def act(Z):
    return [np.maximum(z, 0) * C for z in Z]
def setup_inputs(rng):
    def f(*shape):
        return mx_ref.flush((rng.standard_normal(shape, dtype=np.float32) * np.exp2(rng.integers(-2, 3, shape[:-1] + (1,)))).astype(BF))
    return {"x": f(N, 128, 4 * NC), "w1": f(N, 128, G * 512), "w2": f(N, 128, 512)}
def setup_inputs_blocks(rng):
    d = setup_inputs(rng)
    for k in ("x", "w1", "w2"): d[k] = mx_ref.spread(d[k], rng, 4)
    return d
def setup_inputs_wide(rng):
    d = setup_inputs(rng)
    for k in ("x", "w1", "w2"): d[k] = mx_ref.flush((d[k].astype(np.float32) * np.exp2(rng.integers(-8, 9, (N, 1, 1))).astype(np.float32)).astype(BF))
    return d
def setup_inputs_zeros(rng):
    d = setup_inputs(rng); v = d["x"].reshape(N, 128, -1, 4).copy()
    v[np.broadcast_to((rng.random((N, 1, v.shape[2], 1)) < 0.33), v.shape)] = 0
    d["x"] = v.reshape(d["x"].shape)
    return d
def reference(x, w1, w2):
    y = np.zeros((N, 128, NC), np.float32)
    for e in range(N):
        t = np.concatenate([x[j][:, 4 * OFF[j][e]:4 * OFF[j][e + 1]] for j in range(N)], axis=1)
        p = mx_ref.matmul(mx_ref.quantize(w2[e]), mx_ref.quantize(tile(act(layer(w1[e], [mx_ref.quantize(t)])))))
        c = 0
        for j in range(N):
            a, b = OFF[j][e], OFF[j][e + 1]
            y[j][:, a:b] = p[:, c:c + b - a]; c += b - a
    return {"y": y}

import numpy as np
from concourse.bass import DstId, RemoteDMATransfer
from concourse.mybir import dt, AluOpType, ActivationFunctionType

NC = 256
G = 4
TILE = 256
LEAST = 128
BANK = 512
SCALE = float(np.float32(0.043))

SCRATCH = {
    "xb": ("sbuf", [128, 4 * NC], "bfloat16"),
    "w1b": ("sbuf", [128, G * 512], "bfloat16"),
    "w2b": ("sbuf", [128, 512], "bfloat16"),
    "xq": ("sbuf", [128, 3 * NC], "float8_e4m3fn_x4"),
    "xs": ("sbuf", [128, 3 * NC], "uint8"),
    "w1q": ("sbuf", [128, G * 128], "float8_e4m3fn_x4"),
    "w1s": ("sbuf", [128, G * 128], "uint8"),
    "w2q": ("sbuf", [128, 128], "float8_e4m3fn_x4"),
    "w2s": ("sbuf", [128, 128], "uint8"),
    "h0": ("sbuf", [128, 4 * NC], "bfloat16"),
    "h1": ("sbuf", [128, 4 * NC], "bfloat16"),
    "hq0": ("sbuf", [128, NC], "float8_e4m3fn_x4"),
    "hq1": ("sbuf", [128, NC], "float8_e4m3fn_x4"),
    "hs0": ("sbuf", [128, NC], "uint8"),
    "hs1": ("sbuf", [128, NC], "uint8"),
    "ps": ("psum", [128, 2 * G * BANK], "float32"),
    "pb0": ("sbuf", [128, NC], "float32"),
    "pb1": ("sbuf", [128, NC], "float32"),
    "yb": ("sbuf", [128, NC], "float32"),
}
SEMAPHORES = (["lx", "lw1", "lw2", "qx", "qw2", "afar", "anear", "rfar", "rnear", "sent", "own", "sfar", "snear"]
              + ["qw1%d" % b for b in range(G)]
              + ["z%d%d" % (k, b) for k in range(2) for b in range(G)]
              + ["%s%d" % (s, k) for s in ("act", "qh", "pm", "cp") for k in range(2)])


def _is_far(topo, a, b):
    return (topo.host(a), topo.chip(a)) != (topo.host(b), topo.chip(b))


def _layout(e, cnt, off, cores, topo):
    n = len(cores)
    far = [j for j in range(n) if j != e and cnt[j][e] and _is_far(topo, cores[j], cores[e])]
    near = [j for j in range(n) if j != e and cnt[j][e] and not _is_far(topo, cores[j], cores[e])]
    own, a = cnt[e][e], off[e][e]
    b = a + own
    own_left = own > 0 and a <= NC - b
    best = None
    for left, right in ((far, near), (near, far)):
        groups = []
        for side, srcs in (("l", left), ("r", right)):
            w = sum(cnt[j][e] for j in srcs)
            has_own = own > 0 and (own_left == (side == "l"))
            if not w and not has_own:
                continue
            reach = (b if side == "l" else NC - a) if has_own else 0
            reach = max(reach, LEAST - w)
            if side == "l":
                z0 = TILE - w
                r0, r1 = z0, TILE + reach
            else:
                z0 = TILE + NC
                r0, r1 = z0 - reach, z0 + w
            pieces, p = [], z0
            for j in srcs:
                pieces.append((j, p, cnt[j][e]))
                p += cnt[j][e]
            groups.append({"far": srcs is far, "r0": r0, "r1": r1, "n": r1 - r0, "z0": z0, "w": w, "pieces": pieces,
                           "own": TILE + a if has_own else None})
        groups.sort(key=lambda q: not q["far"])
        cost = (sum(q["n"] for q in groups), groups[0]["n"])
        if best is None or cost < best[0]:
            best = (cost, groups)
    for q in best[1]:
        assert LEAST <= q["n"] <= NC and q["n"] % 2 == 0 and q["r0"] % 2 == 0 and 0 <= q["r0"] and q["r1"] <= 3 * NC
    return best[1]


def _engines(c, cores, topo):
    far = [topo.mask(c, d) for d in cores if d != c and _is_far(topo, c, d)]
    near = [topo.mask(c, d) for d in cores if d != c and not _is_far(topo, c, d)]
    fm = far[0] if far else 0
    nm = near[0] if near else 0
    return fm, (nm & ~fm) or nm, nm


def _split(mask, k):
    bits = [i for i in range(mask.bit_length()) if (mask >> i) & 1]
    per = 1
    while per * 2 * k <= len(bits):
        per *= 2
    return [sum(1 << i for i in bits[t * per:(t + 1) * per]) for t in range(k)], per


def _calls(items, mask, kinds, sem):
    calls, todo = [], sorted(items)
    while todo:
        same = [t for t in todo if t[4] == todo[0][4]]
        todo = [t for t in todo if t[4] != same[0][4]]
        parts, per = _split(mask, len(same))
        for kind in kinds:
            calls.append([{"dst": t[1], "kind": kind, "s0": t[2], "d0": t[3], "w": t[4], "mask": m, "eng": per, "sem": sem}
                          for t, m in zip(same, parts)])
    return calls


def _dispatch(j, lay, cnt, off, cores, topo):
    fm, rest, _ = _engines(cores[j], cores, topo)
    calls = []
    for far, mask, sem in ((True, fm, "afar"), (False, rest, "anear")):
        items = []
        for e in range(len(cores)):
            for q in lay[e]:
                for (src, pos, w) in q["pieces"]:
                    if src == j and q["far"] == far:
                        items.append((-q["n"], e, TILE + off[j][e], pos, w))
        calls += _calls(items, mask, ("codes", "scales"), sem)
    return calls


def _combine(e, lay, off, cores, topo):
    fm, rest, allm = _engines(cores[e], cores, topo)
    any_far = any(q["far"] and q["pieces"] for q in lay[e])
    out = []
    for k, q in enumerate(lay[e]):
        items = [(-w, j, pos - q["z0"], off[j][e], w) for (j, pos, w) in q["pieces"]]
        mask = fm if q["far"] else (rest if any_far else allm)
        out.append(_calls(items, mask, ("p%d" % k,), "rfar" if q["far"] else "rnear"))
    return out


def _landing(all_calls, rank, sem):
    return sum(t["eng"] for calls in all_calls for call in calls for t in call if t["dst"] == rank and t["sem"] == sem)


def rank_program(g, core, T, topo):
    rank = T.rank_of(core)
    if rank is None:
        return
    cores, cnt = list(T.cores), T.tables["CNT"]
    n = len(cores)
    off = [[sum(r[:e]) for e in range(n + 1)] for r in cnt]
    lay = [_layout(e, cnt, off, cores, topo) for e in range(n)]
    disp = [_dispatch(j, lay, cnt, off, cores, topo) for j in range(n)]
    comb = [_combine(e, lay, off, cores, topo) for e in range(n)]
    flat = [[c for grp in comb[e] for c in grp] for e in range(n)]
    groups = lay[rank]
    S = T.sem
    sent = [0]

    def sides(t):
        a, b, w = t["s0"], t["d0"], t["w"]
        if t["kind"] == "codes":
            return T.xq[:, a:a + w].bitcast(dt.uint8), T.xq[:, b:b + w].bitcast(dt.uint8)
        if t["kind"] == "scales":
            return T.xs[:, a:a + w], T.xs[:, b:b + w]
        return T["pb" + t["kind"][1:]][:, a:a + w], T.yb[:, b:b + w]

    def issue(call):
        trs = []
        for t in call:
            d = cores[t["dst"]]
            assert topo.may_write(core, d)
            rid, pid = topo.addr(d, core)
            src, dst = sides(t)
            sent[0] += t["eng"]
            if len(call) == 1:
                g.remote_dma(out_ap=dst, in_ap=src, remote_sem=S[t["sem"]], local_sem=S.sent, pid=pid, routing_id=rid,
                             dma_engine_mask=t["mask"])
                return
            trs.append(RemoteDMATransfer(dst_ids=[DstId(rid=rid, pnc=pid)], dma_engine_mask=t["mask"], remote_sem=S[t["sem"]],
                                         src=src, dst=dst))
        g.remote_dma_fused(trs, local_sem=S.sent)

    g.sync.dma_start(T.xb[:], T.x[:]).then_inc(S.lx, 16)
    g.sync.dma_start(T.w1b[:], T.w1[:]).then_inc(S.lw1, 16)
    g.sync.dma_start(T.w2b[:], T.w2[:]).then_inc(S.lw2, 16)

    v, s, t_ = g.vector, g.scalar, g.tensor
    v.wait_ge(S.lx, 16)
    v.quantize_mx(T.xq[:, TILE:TILE + NC], T.xs[:, TILE:TILE + NC], T.xb[:]).then_inc(S.qx, 1)
    v.wait_ge(S.lw1, 16)
    for b in range(G):
        v.quantize_mx(T.w1q[:, 128 * b:128 * b + 128], T.w1s[:, 128 * b:128 * b + 128],
                      T.w1b[:, 512 * b:512 * b + 512]).then_inc(S["qw1%d" % b], 1)

    g.wait_ge(S.qx, 1)
    for call in disp[rank]:
        issue(call)

    for k, q in enumerate(groups):
        m, r0, r1 = q["n"], q["r0"], q["r1"]
        h, hq, hs, pb = T["h%d" % k], T["hq%d" % k], T["hs%d" % k], T["pb%d" % k]
        base = k * G * BANK
        if q["pieces"]:
            name = "afar" if q["far"] else "anear"
            t_.wait_ge(S[name], _landing(disp, rank, name))
        if r0 < TILE + NC and r1 > TILE:
            t_.wait_ge(S.qx, 1)
        for b in range(G):
            if k == 0:
                t_.wait_ge(S["qw1%d" % b], 1)
            t_.matmul_mx(T.ps[:, base + b * BANK:base + b * BANK + m], T.w1q[:, 128 * b:128 * b + 128],
                         T.w1s[:, 128 * b:128 * b + 128], T.xq[:, r0:r1], T.xs[:, r0:r1], True, True).then_inc(S["z%d%d" % (k, b)], 1)
        for b in range(G):
            z = T.ps[:, base + b * BANK:base + b * BANK + m]
            if b % 2 == 0:
                v.wait_ge(S["z%d%d" % (k, b)], 1)
                v.tensor_scalar(h[:, b:4 * m:4], z, 0.0, SCALE, AluOpType.max, AluOpType.mult).then_inc(S["act%d" % k], 1)
                if k == 0 and b == 0:
                    v.wait_ge(S.lw2, 16)
                    v.quantize_mx(T.w2q[:], T.w2s[:], T.w2b[:]).then_inc(S.qw2, 1)
            else:
                s.wait_ge(S["z%d%d" % (k, b)], 1)
                s.activation(h[:, b:4 * m:4], z, ActivationFunctionType.Relu, scale=SCALE).then_inc(S["act%d" % k], 1)
        v.wait_ge(S["act%d" % k], G)
        v.quantize_mx(hq[:, 0:m], hs[:, 0:m], h[:, 0:4 * m]).then_inc(S["qh%d" % k], 1)
        t_.wait_ge(S["qh%d" % k], 1)
        if k == 0:
            t_.wait_ge(S.qw2, 1)
        t_.matmul_mx(T.ps[:, base:base + m], T.w2q[:], T.w2s[:], hq[:, 0:m], hs[:, 0:m], True, True).then_inc(S["pm%d" % k], 1)
        s.wait_ge(S["pm%d" % k], 1)
        if q["pieces"]:
            c0 = base + q["z0"] - r0
            s.activation(pb[:, 0:q["w"]], T.ps[:, c0:c0 + q["w"]], ActivationFunctionType.Copy).then_inc(S["cp%d" % k], 1)
        if q["own"] is not None:
            c0 = base + q["own"] - r0
            s.activation(T.yb[:, off[rank][rank]:off[rank][rank + 1]], T.ps[:, c0:c0 + cnt[rank][rank]],
                         ActivationFunctionType.Copy).then_inc(S.own, 1)
        if q["pieces"]:
            g.wait_ge(S["cp%d" % k], 1)
            for call in comb[rank][k]:
                issue(call)
    g.wait_ge(S.sent, sent[0])

    for far, queue, arrived, stored in ((True, g.sync, "rfar", "sfar"), (False, g.scalar, "rnear", "snear")):
        segs = []
        for e in range(n):
            if cnt[rank][e] and (e != rank and _is_far(topo, cores[e], core)) == far:
                if segs and segs[-1][1] == off[rank][e]:
                    segs[-1][1] = off[rank][e + 1]
                else:
                    segs.append([off[rank][e], off[rank][e + 1]])
        if not segs:
            continue
        landing = _landing(flat, rank, arrived)
        if landing:
            queue.wait_ge(S[arrived], landing)
        if not far and cnt[rank][rank]:
            queue.wait_ge(S.own, 1)
        for a, b in segs:
            queue.dma_start(T.y[:, a:b], T.yb[:, a:b]).then_inc(S[stored], 16)
        queue.wait_ge(S[stored], 16 * len(segs))
